import numpy as np, ml_dtypes
CORES = [169,41,209,81,249,121]
N = 6
KB, QP = 4, 128
def setup_inputs(rng):
    return {"q": rng.standard_normal((N, 128, QP), dtype=np.float32).astype(ml_dtypes.bfloat16), "k": rng.standard_normal((N, 128, KB * 128), dtype=np.float32).astype(ml_dtypes.bfloat16), "v": rng.standard_normal((N, 128, KB * 128), dtype=np.float32).astype(ml_dtypes.bfloat16)}
def reference(q, k, v):
    Q, K, V = q.astype(np.float64), k.astype(np.float64), v.astype(np.float64)
    y = np.zeros((N, 128, QP))
    for r in range(N):
        for j in range(N):
            for b in range(KB):
                S = np.maximum(K[j][:, 128 * b:128 * b + 128].T @ Q[r], 0.0)
                y[r] += V[j][:, 128 * b:128 * b + 128].T @ S
    return {"y": y.astype(ml_dtypes.bfloat16 if q.dtype != np.float64 else np.float64)}

from concourse.bass import DstId, RemoteDMATransfer
from concourse.mybir import AluOpType

NR, KB, W = 6, 4, 128
QPH = 2
MAXQ = 4

SCRATCH = {
    "qin": ("sbuf", [128, NR * W], "bfloat16"),
    "qd": ("dram", [128, W], "bfloat16"),
    "kv": ("sbuf", [128, 2 * KB * W], "bfloat16"),
    "zero": ("sbuf", [128, 2 * W], "float32"),
    "ssb": ("sbuf", [128, MAXQ * KB * W], "bfloat16"),
    "osb": ("sbuf", [128, NR * W], "bfloat16"),
    "land": ("sbuf", [128, NR * W], "bfloat16"),
    "ysb": ("sbuf", [128, W], "bfloat16"),
}
for _i in range(4):
    SCRATCH["ps%d" % _i] = ("psum", [128, 512], "float32")
    SCRATCH["po%d" % _i] = ("psum", [128, 512], "float32")

SEMAPHORES = ["ldq", "ldd", "ldk", "ldv", "z", "kva", "qr", "sent", "st"]
SEMAPHORES += ["qa%d" % _i for _i in range(NR)] + ["la%d" % _i for _i in range(NR)] + ["ad%d" % _i for _i in range(NR)]
for _i in range(MAXQ):
    SEMAPHORES += ["sS%d0" % _i, "sS%d1" % _i, "sR%d0" % _i, "sR%d1" % _i, "sO%d" % _i, "sE%d" % _i]


def _n(mask):
    return bin(mask).count("1")


def _plan(T, topo):
    ranks = list(T.cores)
    n = len(ranks)
    span = topo.CORES_PER_CHIP
    direct = [[a == b or topo.may_write(ranks[a], ranks[b]) for b in range(n)] for a in range(n)]
    grp = [[b for b in range(n) if direct[a][b]] for a in range(n)]
    idx = [grp[a].index(a) for a in range(n)]
    gates, relays = [], []
    for a in range(n):
        c = ranks[a]
        chip = [d for d in range(max(0, c - span + 1), c + span)
                if d != c and topo.host(d) == topo.host(c) and topo.chip(d) == topo.chip(c)]
        able = [d for d in chip if all(topo.may_write(d, x) for x in ranks)]
        dies = sorted(set(topo.die(d) for d in able))
        pools = [[d for d in able if topo.die(d) == e] for e in dies]
        far = n - len(grp[a])
        hs, t = [], idx[a]
        while len(hs) < len(able):
            pool = pools[t % len(dies)]
            if pool:
                hs.append(pool.pop(0))
            t += 1
        ng = min(len(able), max(1, -(-far // QPH)))
        gates.append(hs[:ng])
        relays.append(hs[:max(ng, min(len(able), far))])
    comp, relay, lc, lr = {}, {}, {}, {}
    for r in range(n):
        for j in range(n):
            if direct[r][j]:
                comp[(r, j)] = ranks[j]
                continue
            best = min((topo.die(a) != topo.die(b), lc.get(b, 0), lr.get(a, 0), a, b)
                       for a in relays[r] for b in gates[j])
            a, b = best[3], best[4]
            comp[(r, j)], relay[(r, j)] = b, a
            lc[b], lr[a] = lc.get(b, 0) + 1, lr.get(a, 0) + 1
    turn, taken, fan = {}, {}, {}
    for r in range(n):
        for a in relays[r]:
            js = [j for j in range(n) if relay.get((r, j)) == a]
            if not js:
                continue
            rots = [js[t:] + js[:t] for t in range(len(js))]
            rot = min(rots, key=lambda o: sum(taken.get((comp[(r, j)], s), 0) for s, j in enumerate(o)))
            for s, j in enumerate(rot):
                turn[(r, j)] = s
                taken[(comp[(r, j)], s)] = taken.get((comp[(r, j)], s), 0) + 1
            fan[a] = (r, rot)
    work, home = {}, {}
    for j in range(n):
        m = len(grp[j])
        work[ranks[j]] = [grp[j][(idx[j] + t) % m] for t in range(m)]
        home[ranks[j]] = j
        for b in relays[j]:
            rs = [r for r in range(n) if comp[(r, j)] == b]
            rs = rs[idx[j] % max(1, len(rs)):] + rs[:idx[j] % max(1, len(rs))]
            work[b] = sorted(rs, key=lambda r: turn[(r, j)])
            home[b] = j
    lo = [topo.mask(ranks[r], ranks[[x for x in grp[r] if x != r][0]]) for r in range(n)]
    hi = [topo.mask(ranks[r], gates[r][0]) & ~lo[r] for r in range(n)]
    return dict(ranks=ranks, grp=grp, gates=gates, relays=relays, comp=comp, relay=relay, fan=fan, work=work,
                home=home, lo=lo, hi=hi)


def _to(topo, dst, src):
    rid, pid = topo.addr(dst, src)
    return DstId(rid=rid, pnc=pid)


def rank_program(g, core, T, topo):
    pl = _plan(T, topo)
    if core not in pl["work"]:
        return
    ranks, work, sem = pl["ranks"], pl["work"], T.sem
    j = pl["home"][core]
    me = T.rank_of(core)
    qs = work[core]
    pe, ve = g.tensor, g.vector
    sent = 0

    def slot(t, s, w=1):
        return t[:, s * W:(s + w) * W]

    kvmask = topo.mask(ranks[j], pl["gates"][j][0])

    if me is not None:
        g.sync.dma_start(T.qd[:, :], T.q[:, :]).then_inc(sem.ldd, 16)
        g.scalar.dma_start(slot(T.qin, me), T.q[:, :]).then_inc(sem.ldq, 16)
        g.sync.dma_start(slot(T.kv, 0, KB), T.k[:, :]).then_inc(sem.ldk, 16)
        g.scalar.dma_start(slot(T.kv, KB, KB), T.v[:, :]).then_inc(sem.ldv, 16)

    def s_step(i):
        r = qs[i]
        if r == me:
            pe.wait_ge(sem.ldq, 16)
        elif me is not None:
            pe.wait_ge(sem["qa%d" % r], _n(pl["lo"][r]))
        else:
            pe.wait_ge(sem["qa%d" % r], _n(topo.mask(pl["relay"][(r, j)], core)))
        if i == 0:
            if me is not None:
                pe.wait_ge(sem.ldk, 16)
            else:
                pe.wait_ge(sem.kva, _n(kvmask))
        for h in range(2):
            bank = T["ps%d" % ((i % 2) * 2 + h)]
            for u in range(2):
                pe.matmul(slot(bank, u), slot(T.kv, 2 * h + u), slot(T.qin, r),
                          start=True, stop=True).then_inc(sem["sS%d%d" % (i, h)], 1)

    def r_step(i):
        for h in range(2):
            bank = T["ps%d" % ((i % 2) * 2 + h)]
            ve.wait_ge(sem["sS%d%d" % (i, h)], 2)
            ve.tensor_tensor(out=slot(T.ssb, i * KB + 2 * h, 2), in0=slot(bank, 0, 2), in1=T.zero[:, :],
                             op=AluOpType.max).then_inc(sem["sR%d%d" % (i, h)], 1)

    def o_step(i):
        if i == 0 and me is not None:
            pe.wait_ge(sem.ldv, 16)
        for h in range(2):
            pe.wait_ge(sem["sR%d%d" % (i, h)], 1)
            for b in (2 * h, 2 * h + 1):
                pe.matmul(slot(T["po%d" % i], 0), slot(T.kv, KB + b), slot(T.ssb, i * KB + b),
                          start=(b == 0), stop=(b == KB - 1)).then_inc(sem["sO%d" % i], 1)

    def e_step(i):
        if qs[i] != me:
            ve.wait_ge(sem["sO%d" % i], KB)
            ve.tensor_copy(out=slot(T.osb, qs[i]), in_=slot(T["po%d" % i], 0)).then_inc(sem["sE%d" % i], 1)

    if qs:
        ve.memset(T.zero[:, :], 0.0).then_inc(sem.z, 1)
        ve.wait_ge(sem.z, 1)
    ahead = 1 if me is None else 0
    for i in range(len(qs) + ahead):
        if i < len(qs):
            s_step(i)
            r_step(i)
        if i >= ahead:
            o_step(i - ahead)
            e_step(i - ahead)

    if me is not None:
        peers = sorted((x for x in pl["grp"][me] if x != me), key=lambda x: work[ranks[x]].index(me))
        hs = [a for a in pl["relays"][me] if a in pl["fan"]]
        g.wait_ge(sem.ldd, 16)
        g.remote_dma_fused([
            RemoteDMATransfer(dst_ids=[_to(topo, a, core) for a in hs], dma_engine_mask=pl["hi"][me],
                              remote_sem=sem.qr, srcs=[T.qd[:, :]], dsts=[T.qd[:, :] for a in hs]),
            RemoteDMATransfer(dst_ids=[_to(topo, ranks[x], core) for x in peers], dma_engine_mask=pl["lo"][me],
                              remote_sem=sem["qa%d" % me], srcs=[T.qd[:, :]], dsts=[slot(T.qin, me) for x in peers]),
        ], local_sem=sem.sent)
        sent += _n(pl["hi"][me]) + _n(pl["lo"][me])
        gs = pl["gates"][me]
        g.wait_ge(sem.ldk, 16)
        g.wait_ge(sem.ldv, 16)
        g.remote_dma_fused([RemoteDMATransfer(dst_ids=[_to(topo, a, core) for a in gs], dma_engine_mask=kvmask,
                                              remote_sem=sem.kva, srcs=[T.kv[:, :]], dsts=[T.kv[:, :] for a in gs])],
                           local_sem=sem.sent)
        sent += _n(kvmask)
    elif core in pl["fan"]:
        r0, js = pl["fan"][core]
        dsts = [pl["comp"][(r0, x)] for x in js]
        m = topo.mask(core, dsts[0])
        g.wait_ge(sem.qr, _n(pl["hi"][r0]))
        g.remote_dma_fused([RemoteDMATransfer(dst_ids=[_to(topo, d, core) for d in dsts], dma_engine_mask=m,
                                              remote_sem=sem["qa%d" % r0], srcs=[T.qd[:, :]],
                                              dsts=[slot(T.qin, r0) for d in dsts])], local_sem=sem.sent)
        sent += _n(m)

    for i, r in enumerate(qs):
        if r == me:
            continue
        rid, pid = topo.addr(ranks[r], core)
        m = topo.mask(core, ranks[r])
        g.wait_ge(sem["sE%d" % i], 1)
        g.remote_dma(out_ap=slot(T.land, j), in_ap=slot(T.osb, r), remote_sem=sem["la%d" % j], local_sem=sem.sent,
                     pid=pid, routing_id=rid, dma_engine_mask=m)
        sent += _n(m)
    g.wait_ge(sem.sent, sent)

    if me is not None:
        others = sorted((x for x in range(len(ranks)) if x != me),
                        key=lambda x: (pl["comp"][(me, x)] != ranks[x], work[pl["comp"][(me, x)]].index(me), x))
        acc = slot(T.po0, 0)
        ve.wait_ge(sem.sO0, KB)
        for t, x in enumerate(others):
            ve.wait_ge(sem["la%d" % x], _n(topo.mask(pl["comp"][(me, x)], core)))
            if t:
                ve.wait_ge(sem["ad%d" % (t - 1)], 1)
            last = t == len(others) - 1
            ve.tensor_tensor(out=T.ysb[:, :] if last else acc, in0=acc, in1=slot(T.land, x),
                             op=AluOpType.add).then_inc(sem["ad%d" % t], 1)
        g.sync.wait_ge(sem["ad%d" % (len(others) - 1)], 1)
        g.sync.dma_start(T.y[:, :], T.ysb[:, :]).then_inc(sem.st, 16)
        g.sync.wait_ge(sem.st, 16)
